import numpy as np
import ml_dtypes


def mxq(x, axis, fmt="e4m3"):
    dtype, down = {"e4m3": (ml_dtypes.float8_e4m3fn, 7), "e5m2": (ml_dtypes.float8_e5m2, 14)}[fmt]
    v = np.moveaxis(np.asarray(x, np.float32).astype(ml_dtypes.bfloat16).astype(np.float64), axis, -1)
    blocks = v.reshape(v.shape[:-1] + (-1, 32))
    amax = np.abs(blocks).max(-1, keepdims=True)
    byte = np.maximum(np.where(amax > 0, np.frexp(amax)[1] - 1 + 127, 0) - down, 1)
    scale = np.exp2(byte - 127.0)
    codes = (blocks / scale).astype(np.float32).astype(dtype).astype(np.float64)
    return np.moveaxis((codes * scale).reshape(v.shape), -1, axis)


WIDE = False


def mx_kscale(k):
    if not WIDE:
        return np.ones(k)
    levels = np.array([10, -10, 5, -5, 0])
    if k % 512:
        return np.exp2(np.random.permutation(np.resize(levels, k // 32))).repeat(32)
    a = np.empty((k // 512, 16))
    for p in range(k // 512):
        a[p, :8] = np.random.permutation(np.resize(levels, 8))
        for g in range(8):
            far = levels[np.abs(levels - a[p, g]) >= 10]
            a[p, g + 8] = far[np.random.randint(len(far))]
    return np.exp2(a.ravel()).repeat(32)


def f64(x):
    return np.asarray(x).astype(np.float64)


def striped(idx):
    return np.tile(np.asarray(idx).reshape(-1, 16).T, (8, 1)).astype(np.uint16)


def unstriped(offs):
    return offs[:16].T.reshape(-1).astype(np.int64)


E2M1 = np.array([0.0, 0.5, 1.0, 1.5, 2.0, 3.0, 4.0, 6.0, -0.0, -0.5, -1.0, -1.5, -2.0, -3.0, -4.0, -6.0])


def pack_weight(w, fmt):
    k, n = w.shape
    w = f64(np.asarray(w, np.float32).astype(ml_dtypes.bfloat16)).reshape(k // 32, 32, n)
    amax = np.abs(w).max(1)
    if fmt == "e4m3":
        byte = np.frexp(amax)[1] - 1 + 127 - 7
    else:
        mant, ex = np.frexp(amax / 6.0)
        byte = np.where(mant > 0.5, ex, ex - 1) + 127
    byte = np.clip(np.where(amax > 0, byte, 1), 1, 254)
    scaled = (w * np.exp2(127.0 - byte)[:, None, :]).reshape(k, n).astype(np.float32)
    by_word = np.ascontiguousarray(scaled.reshape(k // 512, 128, 4, n).transpose(0, 1, 3, 2))
    if fmt == "e4m3":
        words = by_word.astype(ml_dtypes.float8_e4m3fn).view(np.uint8)
    else:
        c = by_word.astype(ml_dtypes.float4_e2m1fn).view(np.uint8) & 0xF
        words = (c[..., 0::2] | (c[..., 1::2] << 4)).reshape(k // 512, 128, 2 * n)
    return np.ascontiguousarray(words), np.ascontiguousarray(byte.astype(np.uint8).reshape(k // 512, 16, n))


def unpack_weight(words, scales, fmt):
    g, _, n = scales.shape
    words = np.ascontiguousarray(words).reshape(g, 128, n, -1)
    if fmt == "e4m3":
        vals = words.view(ml_dtypes.float8_e4m3fn).astype(np.float64)
    else:
        nib = np.empty((g, 128, n, 4), np.uint8)
        nib[..., 0::2] = words & 0xF
        nib[..., 1::2] = words >> 4
        vals = E2M1[nib]
    vals = vals * np.repeat(np.exp2(scales.astype(np.float64) - 127.0), 8, axis=1)[..., None]
    return vals.transpose(0, 1, 3, 2).reshape(g * 512, n)


def bf(x):
    return np.asarray(x, np.float32).astype(ml_dtypes.bfloat16)


def planes(Y):
    r, m = Y.shape
    b = f64(bf(Y)).reshape(r // 32, 32, m)
    amax = np.abs(b).max(1)
    byte = np.clip(np.where(amax > 0, np.frexp(amax)[1] - 1 + 127 - 7, 1), 1, 254)
    codes = (b * np.exp2(127.0 - byte)[:, None, :]).reshape(r, m).astype(np.float32).astype(ml_dtypes.float8_e4m3fn).view(np.uint8)
    words = codes.reshape(r // 512, 128, 4, m).transpose(0, 1, 3, 2)
    return np.ascontiguousarray(words), np.ascontiguousarray(byte.astype(np.uint8).reshape(r // 512, 16, m))


D, K, T, I, J, Q = 512, 512, 2048, 1024, 512, 512


def setup_inputs():
    n = np.random.standard_normal
    idx = np.random.permutation(T)[:I]
    idx2 = np.random.randint(0, I, J)
    idx3 = np.random.randint(0, I, J)
    idx4 = np.random.randint(0, I, J)
    fd = mx_kscale(D)
    fk = mx_kscale(K)
    etp = pack_weight(n((D, T)) / fd[:, None], "e4m3")
    edp = pack_weight(n((K, T)) / fk[:, None], "e4m3")
    return {
        "ht": (n((D, Q)) * 0.6 / np.sqrt(D) * fd[:, None]).astype(np.float32),
        "hd": (n((K, Q)) * 0.6 / np.sqrt(K) * fk[:, None]).astype(np.float32),
        "et_words": etp[0],
        "et_scales": etp[1],
        "ed_words": edp[0],
        "ed_scales": edp[1],
        "l1": (np.random.uniform(7.0, 7.3, (Q, 1))).astype(np.float32),
        "l2": (np.random.uniform(7.0, 7.3, (Q, 1))).astype(np.float32),
        "offs": striped(idx),
        "offs2": striped(idx2),
        "offs3": striped(idx3),
        "offs4": striped(idx4),
    }


def reference(ht, hd, et_words, et_scales, ed_words, ed_scales, l1, l2, offs, offs2, offs3, offs4):
    idx = unstriped(offs)
    idx2 = unstriped(offs2)
    idx3 = unstriped(offs3)
    idx4 = unstriped(offs4)
    etu = unpack_weight(et_words, et_scales, "e4m3")
    edu = unpack_weight(ed_words, ed_scales, "e4m3")
    htq = mxq(f64(ht), 0, "e4m3")
    etidxg = etu[:, idx]
    a = htq.T @ etidxg
    hdq = mxq(f64(hd), 0, "e4m3")
    edidxg = edu[:, idx]
    b = hdq.T @ edidxg
    r = np.minimum(np.exp(a - f64(l1) - b + f64(l2)), 1.0)
    y = r[:, idx2] * (r[:, idx3] * (r[:, idx4] + 1.0) + 1.0)
    words, scales = planes(y)
    return y, words, scales

@@ -1,0 +1,162 @@
+from contextlib import ExitStack
+
+import concourse.mybir as mybir
+
+D, K, T, I, J, Q = 512, 512, 2048, 1024, 512, 512
+FLOPS = 2 * Q * I * (D + K)
+
+F32 = mybir.dt.float32
+BF16 = mybir.dt.bfloat16
+I32 = mybir.dt.int32
+U32 = mybir.dt.uint32
+U16 = mybir.dt.uint16
+U8 = mybir.dt.uint8
+FP8X4 = mybir.dt.float8_e4m3fn_x4
+ALU = mybir.AluOpType
+ACT = mybir.ActivationFunctionType
+
+P = 128
+PACK = 4
+BANK = 512
+HD_PIECES = ((0, 96), (96, 128))
+HALF = J // 2
+
+
+def load_scale_rows(queue, window, scales):
+    for quad in range(4):
+        queue.dma_start(
+            out=window[32 * quad : 32 * quad + 4, :].bitcast(I32),
+            in_=scales[0, 4 * quad : 4 * quad + 4, :].bitcast(I32),
+        )
+
+
+def tile_attend_acceptedlength_pl_kernel(
+    tc, ht, hd, et_words, et_scales, ed_words, ed_scales, l1, l2, offs, offs2, offs3, offs4, out_0, out_1, out_2
+):
+    nc = tc.nc
+    with ExitStack() as ctx:
+        lists = ctx.enter_context(tc.tile_pool(name="lists", bufs=1))
+        keep = ctx.enter_context(tc.tile_pool(name="keep", bufs=1))
+        psum = ctx.enter_context(tc.psum_pool(name="psum", bufs=1))
+
+        nodes = lists.tile([P, I // 16], U16, name="nodes")
+        first = lists.tile([P, J // 16], U16, name="first")
+        second = lists.tile([P, J // 16], U16, name="second")
+        third = lists.tile([P, J // 16], U16, name="third")
+
+        et_w = keep.tile([P, T], I32, name="et_w", align_bytes=64)
+        ed_w = keep.tile([P, T], I32, name="ed_w", align_bytes=64)
+        et_s = keep.tile([P, T], U8, name="et_s", align_bytes=64)
+        ed_s = keep.tile([P, T], U8, name="ed_s", align_bytes=64)
+        ht_raw = keep.tile([P, PACK, Q], F32, name="ht_raw", align_bytes=64)
+        hd_raw = [keep.tile([P, PACK, PACK * (b - a)], F32, name=f"hd_raw{a}", align_bytes=64) for a, b in HD_PIECES]
+        l1_sb = keep.tile([P, PACK], F32, name="l1_sb")
+        l2_sb = keep.tile([P, PACK], F32, name="l2_sb")
+
+        nc.vector.memset(et_s[:].bitcast(I32), 0)
+        nc.gpsimd.memset(ed_s[:].bitcast(I32), 0)
+        nc.sync.dma_start(nodes[:], offs)
+        load_scale_rows(nc.scalar, et_s, et_scales)
+        load_scale_rows(nc.scalar, ed_s, ed_scales)
+        nc.sync.dma_start(out=et_w[:], in_=et_words[0].rearrange("p n r -> p (n r)").bitcast(I32))
+        nc.sync.dma_start(out=ht_raw[:], in_=ht.rearrange("(p j) q -> p j q", j=PACK))
+        nc.sync.dma_start(out=ed_w[:], in_=ed_words[0].rearrange("p n r -> p (n r)").bitcast(I32))
+        for piece, (a, b) in zip(hd_raw, HD_PIECES):
+            nc.sync.dma_start(out=piece[:], in_=hd.rearrange("(p j) q -> p j q", j=PACK)[:, :, PACK * a : PACK * b])
+        nc.gpsimd.dma_start(out=l1_sb[:], in_=l1.rearrange("(p t) o -> p (t o)", t=PACK))
+        nc.gpsimd.dma_start(out=l2_sb[:], in_=l2.rearrange("(p t) o -> p (t o)", t=PACK))
+        nc.sync.dma_start(third[:], offs4)
+        nc.sync.dma_start(first[:], offs2)
+        nc.sync.dma_start(second[:], offs3)
+
+        et_gw = keep.tile([P, I], U32, name="et_gw", align_bytes=64)
+        et_gs = keep.tile([P, I], U8, name="et_gs", align_bytes=64)
+        ed_gs = keep.tile([P, I], U8, name="ed_gs", align_bytes=64)
+        nc.vector.tensor_copy(et_gs[:], et_s[:].indirect(nodes[:]))
+        nc.vector.tensor_copy(et_gw[:], et_w[:].bitcast(U32).indirect(nodes[:]))
+        nc.vector.tensor_copy(ed_gs[:], ed_s[:].indirect(nodes[:]))
+
+        shift = keep.tile([P, PACK], F32, name="shift")
+        nc.gpsimd.tensor_tensor(shift[:], l1_sb[:], l2_sb[:], ALU.subtract)
+
+        ht_b = keep.tile([P, PACK, P, PACK], BF16, name="ht_b", tag="ht_b_then_ed_gw", align_bytes=64)
+        hd_b = keep.tile([P, PACK, P, PACK], BF16, name="hd_b", align_bytes=64)
+        ht_c = keep.tile([P, Q], U32, name="ht_c", align_bytes=64)
+        ht_s = keep.tile([P, Q], U8, name="ht_s", align_bytes=64)
+        hd_c = keep.tile([P, Q], U32, name="hd_c", align_bytes=64)
+        hd_s = keep.tile([P, Q], U8, name="hd_s", align_bytes=64)
+        nc.scalar.activation(
+            ht_b[:].rearrange("p t m j -> p m j t"), ht_raw[:].rearrange("p j (m t) -> p m j t", t=PACK), ACT.Copy
+        )
+        nc.vector.quantize_mx(out=ht_c[:].bitcast(FP8X4), scales=ht_s[:], in_=ht_b[:].rearrange("p t m j -> p (t m j)"))
+        ed_gw = keep.tile([P, I], U32, name="ed_gw", tag="ht_b_then_ed_gw", align_bytes=64)
+        nc.vector.tensor_copy(ed_gw[:], ed_w[:].bitcast(U32).indirect(nodes[:]))
+        for piece, (a, b) in zip(hd_raw, HD_PIECES):
+            nc.scalar.activation(
+                hd_b[:, :, a:b, :].rearrange("p t m j -> p m j t"),
+                piece[:].rearrange("p j (m t) -> p m j t", t=PACK),
+                ACT.Copy,
+                scale=-1.0,
+            )
+
+        r = [keep.tile([P, 2 * I], F32, name=f"r{t}", align_bytes=64) for t in range(PACK)]
+        for t0, t1 in ((0, 1), (1, 2), (2, 4)):
+            nc.vector.quantize_mx(
+                out=hd_c[:, P * t0 : P * t1].bitcast(FP8X4), scales=hd_s[:, P * t0 : P * t1],
+                in_=hd_b[:, t0:t1].rearrange("p t m j -> p (t m j)"),
+            )
+        for t in range(PACK):
+            rows = slice(P * t, P * (t + 1))
+            banks = [psum.tile([P, BANK], F32, name=f"bank{h}", bufs=2) for h in range(I // BANK)]
+            for h_c, h_s, gw, gs in ((ht_c, ht_s, et_gw, et_gs), (hd_c, hd_s, ed_gw, ed_gs)):
+                for h in range(I // BANK):
+                    cols = slice(BANK * h, BANK * (h + 1))
+                    nc.tensor.matmul_mx(
+                        out=banks[h][:], lhsT=h_c[:, rows].bitcast(FP8X4), lhsT_scale=h_s[:, rows],
+                        rhs=gw[:, cols].bitcast(FP8X4), rhs_scale=gs[:, cols], start=h_c is ht_c, stop=h_c is hd_c,
+                    )
+            for h in range(I // BANK):
+                cols, spare = slice(BANK * h, BANK * (h + 1)), slice(I + BANK * h, I + BANK * (h + 1))
+                if t == 0 and h == 1:
+                    nc.vector.tensor_scalar(r[t][:, spare], banks[h][:], shift[:, t : t + 1], 0.0, ALU.subtract, ALU.min)
+                    nc.scalar.activation(r[t][:, cols], r[t][:, spare], ACT.Exp)
+                else:
+                    nc.scalar.activation(r[t][:, spare], banks[h][:], ACT.Relu, bias=shift[:, t : t + 1], scale=-1.0)
+                    nc.scalar.activation(r[t][:, cols], r[t][:, spare], ACT.Exp, scale=-1.0)
+
+        y_b = keep.tile([P, J, PACK], BF16, name="y_b", align_bytes=64)
+        y_c = keep.tile([P, J], U32, name="y_c", align_bytes=64)
+        y_s = keep.tile([P, J], U8, name="y_s", align_bytes=64)
+        out_rows = out_0.rearrange("(p t) j -> p t j", t=PACK)
+        out_words = out_1[0].rearrange("p n r -> p (n r)").bitcast(I32)
+        y23 = keep.tile([P, 2, J], F32, name="y23", align_bytes=64)
+        y01 = keep.tile([P, 2, J], F32, name="y01", align_bytes=64)
+        pairs = (y01, y23)
+        for t in range(PACK):
+            g4 = keep.tile([P, J], F32, name=f"g4{t}", align_bytes=64)
+            g2 = keep.tile([P, J], F32, name=f"g2{t}", align_bytes=64)
+            u = keep.tile([P, J], F32, name=f"u{t}", align_bytes=64)
+            y_t = pairs[t // 2][:, t % 2, :]
+            nc.vector.tensor_scalar(g4[:], r[t][:].indirect(third[:]), 1.0, 1.0, ALU.mult, ALU.add)
+            parts = ((0, J),) if t < PACK - 1 else ((0, HALF), (HALF, J))
+            for a, b in parts:
+                nc.vector.tensor_copy(g2[:, a:b], r[t][:].indirect(first[:, a // 16 : b // 16]))
+                nc.vector.tensor_tensor(u[:, a:b], r[t][:].indirect(second[:, a // 16 : b // 16]), g4[:, a:b], ALU.mult)
+                nc.vector.scalar_tensor_tensor(y_t[:, a:b], u[:, a:b], 1.0, g2[:, a:b], ALU.add, ALU.mult)
+                nc.sync.dma_start(out=out_rows[:, t, a:b], in_=y_t[:, a:b])
+                if t == 1:
+                    nc.scalar.copy(y_b[:, :, 0:2], y01[:].rearrange("p t j -> p j t"))
+                if t == 3:
+                    if a == 0:
+                        nc.scalar.copy(y_b[:, a:b, 2:4], y23[:, :, a:b].rearrange("p t j -> p j t"))
+                    else:
+                        nc.vector.tensor_copy(y_b[:, a:b, 2:4], y23[:, :, a:b].rearrange("p t j -> p j t"))
+                    nc.vector.quantize_mx(
+                        out=y_c[:, a:b].bitcast(FP8X4), scales=y_s[:, a:b], in_=y_b[:, a:b, :].rearrange("p j t -> p (j t)")
+                    )
+                    nc.scalar.dma_start(out=out_words[:, a:b], in_=y_c[:, a:b].bitcast(I32))
+        for quad in range(4):
+            queue = nc.sync if quad % 2 == 0 else nc.scalar
+            queue.dma_start(
+                out=out_2[0, 4 * quad : 4 * quad + 4, :].bitcast(I32), in_=y_s[32 * quad : 32 * quad + 4, :].bitcast(I32)
+            )

@@ -18,8 +18,9 @@ ACT = mybir.ActivationFunctionType
 P = 128
 PACK = 4
 BANK = 512
-HD_PIECES = ((0, 96), (96, 128))
 HALF = J // 2
+WHOLE_BANKS = ((0, BANK), (BANK, I))
+FINE = ((0, BANK), (BANK, BANK + BANK // 2), (BANK + BANK // 2, I))
 
 
 def load_scale_rows(queue, window, scales):
@@ -45,11 +46,11 @@ def tile_attend_acceptedlength_pl_kernel(
         third = lists.tile([P, J // 16], U16, name="third")
 
         et_w = keep.tile([P, T], I32, name="et_w", align_bytes=64)
-        ed_w = keep.tile([P, T], I32, name="ed_w", align_bytes=64)
+        ed_w = keep.tile([P, T], I32, name="ed_w", tag="ed_w_then_late_codes", align_bytes=64)
         et_s = keep.tile([P, T], U8, name="et_s", align_bytes=64)
-        ed_s = keep.tile([P, T], U8, name="ed_s", align_bytes=64)
+        ed_s = keep.tile([P, T], U8, name="ed_s", tag="ed_s_then_early_s", align_bytes=64)
         ht_raw = keep.tile([P, PACK, Q], F32, name="ht_raw", align_bytes=64)
-        hd_raw = [keep.tile([P, PACK, PACK * (b - a)], F32, name=f"hd_raw{a}", align_bytes=64) for a, b in HD_PIECES]
+        hd_raw = keep.tile([P, PACK, Q], F32, name="hd_raw", align_bytes=64)
         l1_sb = keep.tile([P, PACK], F32, name="l1_sb")
         l2_sb = keep.tile([P, PACK], F32, name="l2_sb")
 
@@ -57,12 +58,14 @@ def tile_attend_acceptedlength_pl_kernel(
         nc.gpsimd.memset(ed_s[:].bitcast(I32), 0)
         nc.sync.dma_start(nodes[:], offs)
         load_scale_rows(nc.scalar, et_s, et_scales)
-        load_scale_rows(nc.scalar, ed_s, ed_scales)
+        warm = keep.tile([P, 2], F32, name="warm")
+        nc.vector.memset(warm[:, 0:1], 0.0)
+        nc.scalar.activation(warm[:, 1:2], warm[:, 0:1], ACT.Exp)
         nc.sync.dma_start(out=et_w[:], in_=et_words[0].rearrange("p n r -> p (n r)").bitcast(I32))
         nc.sync.dma_start(out=ht_raw[:], in_=ht.rearrange("(p j) q -> p j q", j=PACK))
+        load_scale_rows(nc.sync, ed_s, ed_scales)
+        nc.sync.dma_start(out=hd_raw[:], in_=hd.rearrange("(p j) q -> p j q", j=PACK))
         nc.sync.dma_start(out=ed_w[:], in_=ed_words[0].rearrange("p n r -> p (n r)").bitcast(I32))
-        for piece, (a, b) in zip(hd_raw, HD_PIECES):
-            nc.sync.dma_start(out=piece[:], in_=hd.rearrange("(p j) q -> p j q", j=PACK)[:, :, PACK * a : PACK * b])
         nc.gpsimd.dma_start(out=l1_sb[:], in_=l1.rearrange("(p t) o -> p (t o)", t=PACK))
         nc.gpsimd.dma_start(out=l2_sb[:], in_=l2.rearrange("(p t) o -> p (t o)", t=PACK))
         nc.sync.dma_start(third[:], offs4)
@@ -77,84 +80,107 @@ def tile_attend_acceptedlength_pl_kernel(
         nc.vector.tensor_copy(ed_gs[:], ed_s[:].indirect(nodes[:]))
 
         shift = keep.tile([P, PACK], F32, name="shift")
-        nc.gpsimd.tensor_tensor(shift[:], l1_sb[:], l2_sb[:], ALU.subtract)
+        for t in range(PACK):
+            nc.scalar.activation(shift[:, t : t + 1], l2_sb[:, t : t + 1], ACT.Identity, bias=l1_sb[:, t : t + 1], scale=-1.0)
 
-        ht_b = keep.tile([P, PACK, P, PACK], BF16, name="ht_b", tag="ht_b_then_ed_gw", align_bytes=64)
-        hd_b = keep.tile([P, PACK, P, PACK], BF16, name="hd_b", align_bytes=64)
-        ht_c = keep.tile([P, Q], U32, name="ht_c", align_bytes=64)
-        ht_s = keep.tile([P, Q], U8, name="ht_s", align_bytes=64)
-        hd_c = keep.tile([P, Q], U32, name="hd_c", align_bytes=64)
-        hd_s = keep.tile([P, Q], U8, name="hd_s", align_bytes=64)
+        ht_b = keep.tile([P, PACK, P, PACK], BF16, name="ht_b", align_bytes=64)
+        hd_b = [keep.tile([P, 2, P, PACK], BF16, name=f"hd_b{i}", align_bytes=64) for i in range(2)]
+        hd_dealt = hd_raw[:].rearrange("p j (m t) -> p m j t", t=PACK)
         nc.scalar.activation(
             ht_b[:].rearrange("p t m j -> p m j t"), ht_raw[:].rearrange("p j (m t) -> p m j t", t=PACK), ACT.Copy
         )
-        nc.vector.quantize_mx(out=ht_c[:].bitcast(FP8X4), scales=ht_s[:], in_=ht_b[:].rearrange("p t m j -> p (t m j)"))
-        ed_gw = keep.tile([P, I], U32, name="ed_gw", tag="ht_b_then_ed_gw", align_bytes=64)
-        nc.vector.tensor_copy(ed_gw[:], ed_w[:].bitcast(U32).indirect(nodes[:]))
-        for piece, (a, b) in zip(hd_raw, HD_PIECES):
+        for i in range(2):
             nc.scalar.activation(
-                hd_b[:, :, a:b, :].rearrange("p t m j -> p m j t"),
-                piece[:].rearrange("p j (m t) -> p m j t", t=PACK),
-                ACT.Copy,
-                scale=-1.0,
+                hd_b[i][:].rearrange("p t m j -> p m j t"), hd_dealt[:, :, :, 2 * i : 2 * i + 2], ACT.Copy, scale=-1.0
             )
 
+        def quantise(codes, scales, pair):
+            nc.vector.quantize_mx(out=codes.bitcast(FP8X4), scales=scales, in_=pair.rearrange("p t m j -> p (t m j)"))
+            return codes, scales
+
+        ht01_c = keep.tile([P, 2 * P], U32, name="ht01_c", align_bytes=64)
+        ht01_s = keep.tile([P, 2 * P], U8, name="ht01_s", tag="ed_s_then_early_s", align_bytes=64)
+        hd01_c = keep.tile([P, 2 * P], U32, name="hd01_c", align_bytes=64)
+        hd01_s = keep.tile([P, 2 * P], U8, name="hd01_s", align_bytes=64)
+        target = [quantise(ht01_c[:], ht01_s[:], ht_b[:, 0:2])]
+        draft = [quantise(hd01_c[:], hd01_s[:], hd_b[0][:])]
+        ed_gw = keep.tile([P, I], U32, name="ed_gw", align_bytes=64)
+        for a, b in FINE:
+            nc.vector.tensor_copy(ed_gw[:, a:b], ed_w[:].bitcast(U32).indirect(nodes[:, a // 16 : b // 16]))
+
         r = [keep.tile([P, 2 * I], F32, name=f"r{t}", align_bytes=64) for t in range(PACK)]
-        for t0, t1 in ((0, 1), (1, 2), (2, 4)):
-            nc.vector.quantize_mx(
-                out=hd_c[:, P * t0 : P * t1].bitcast(FP8X4), scales=hd_s[:, P * t0 : P * t1],
-                in_=hd_b[:, t0:t1].rearrange("p t m j -> p (t m j)"),
-            )
-        for t in range(PACK):
-            rows = slice(P * t, P * (t + 1))
-            banks = [psum.tile([P, BANK], F32, name=f"bank{h}", bufs=2) for h in range(I // BANK)]
-            for h_c, h_s, gw, gs in ((ht_c, ht_s, et_gw, et_gs), (hd_c, hd_s, ed_gw, ed_gs)):
-                for h in range(I // BANK):
-                    cols = slice(BANK * h, BANK * (h + 1))
+        nc.vector.memset(r[0][:, I + BANK :], 0.0)
+
+        def chances(t):
+            pieces = FINE if t == 0 else WHOLE_BANKS
+            if t == 0:
+                banks = [psum.tile([P, b - a], F32, name=f"fine{a}") for a, b in pieces]
+            else:
+                banks = [psum.tile([P, b - a], F32, name=f"bank{a}", bufs=2) for a, b in pieces]
+            for side, gw, gs in ((target, et_gw, et_gs), (draft, ed_gw, ed_gs)):
+                codes, scales = side[t // 2]
+                rows = slice(P * (t % 2), P * (t % 2 + 1))
+                for bank, (a, b) in zip(banks, pieces):
                     nc.tensor.matmul_mx(
-                        out=banks[h][:], lhsT=h_c[:, rows].bitcast(FP8X4), lhsT_scale=h_s[:, rows],
-                        rhs=gw[:, cols].bitcast(FP8X4), rhs_scale=gs[:, cols], start=h_c is ht_c, stop=h_c is hd_c,
+                        out=bank[:], lhsT=codes[:, rows].bitcast(FP8X4), lhsT_scale=scales[:, rows],
+                        rhs=gw[:, a:b].bitcast(FP8X4), rhs_scale=gs[:, a:b],
+                        start=side is target, stop=side is draft,
                     )
-            for h in range(I // BANK):
-                cols, spare = slice(BANK * h, BANK * (h + 1)), slice(I + BANK * h, I + BANK * (h + 1))
-                if t == 0 and h == 1:
-                    nc.vector.tensor_scalar(r[t][:, spare], banks[h][:], shift[:, t : t + 1], 0.0, ALU.subtract, ALU.min)
-                    nc.scalar.activation(r[t][:, cols], r[t][:, spare], ACT.Exp)
+            for bank, (a, b) in zip(banks, pieces):
+                if t == 0 and a > 0:
+                    capped = r[1][:, BANK + a : BANK + b]
+                    nc.vector.tensor_scalar(capped, bank[:], shift[:, t : t + 1], 0.0, ALU.subtract, ALU.min)
+                    nc.scalar.activation(r[t][:, a:b], capped, ACT.Exp)
                 else:
-                    nc.scalar.activation(r[t][:, spare], banks[h][:], ACT.Relu, bias=shift[:, t : t + 1], scale=-1.0)
-                    nc.scalar.activation(r[t][:, cols], r[t][:, spare], ACT.Exp, scale=-1.0)
+                    excess = r[t][:, I + a : I + b]
+                    nc.scalar.activation(excess, bank[:], ACT.Relu, bias=shift[:, t : t + 1], scale=-1.0)
+                    nc.scalar.activation(r[t][:, a:b], excess, ACT.Exp, scale=-1.0)
 
         y_b = keep.tile([P, J, PACK], BF16, name="y_b", align_bytes=64)
         y_c = keep.tile([P, J], U32, name="y_c", align_bytes=64)
         y_s = keep.tile([P, J], U8, name="y_s", align_bytes=64)
         out_rows = out_0.rearrange("(p t) j -> p t j", t=PACK)
         out_words = out_1[0].rearrange("p n r -> p (n r)").bitcast(I32)
-        y23 = keep.tile([P, 2, J], F32, name="y23", align_bytes=64)
-        y01 = keep.tile([P, 2, J], F32, name="y01", align_bytes=64)
-        pairs = (y01, y23)
+        pairs = [keep.tile([P, 2, J], F32, name=f"y_pair{i}", align_bytes=64) for i in range(2)]
+        g4 = [keep.tile([P, J], F32, name=f"g4{t}", align_bytes=64) for t in range(PACK)]
+
+        def inner(t):
+            nc.vector.tensor_scalar(g4[t][:], r[t][:].indirect(third[:]), 1.0, 1.0, ALU.mult, ALU.add)
+
+        chances(0)
+        late_c = keep.tile([P, 4 * P], U32, name="late_c", tag="ed_w_then_late_codes", align_bytes=64)
+        late_s = keep.tile([P, 4 * P], U8, name="late_s", align_bytes=64)
+        target.append(quantise(late_c[:, : 2 * P], late_s[:, : 2 * P], ht_b[:, 2:4]))
+        draft.append(quantise(late_c[:, 2 * P :], late_s[:, 2 * P :], hd_b[1][:]))
+        inner(0)
         for t in range(PACK):
-            g4 = keep.tile([P, J], F32, name=f"g4{t}", align_bytes=64)
-            g2 = keep.tile([P, J], F32, name=f"g2{t}", align_bytes=64)
-            u = keep.tile([P, J], F32, name=f"u{t}", align_bytes=64)
+            last = t == PACK - 1
+            parts = ((0, HALF), (HALF, J)) if last else ((0, J),)
+            u = keep.tile([P, J], F32, name="u", align_bytes=64)
             y_t = pairs[t // 2][:, t % 2, :]
-            nc.vector.tensor_scalar(g4[:], r[t][:].indirect(third[:]), 1.0, 1.0, ALU.mult, ALU.add)
-            parts = ((0, J),) if t < PACK - 1 else ((0, HALF), (HALF, J))
             for a, b in parts:
-                nc.vector.tensor_copy(g2[:, a:b], r[t][:].indirect(first[:, a // 16 : b // 16]))
-                nc.vector.tensor_tensor(u[:, a:b], r[t][:].indirect(second[:, a // 16 : b // 16]), g4[:, a:b], ALU.mult)
-                nc.vector.scalar_tensor_tensor(y_t[:, a:b], u[:, a:b], 1.0, g2[:, a:b], ALU.add, ALU.mult)
+                nc.vector.tensor_tensor(u[:, a:b], r[t][:].indirect(second[:, a // 16 : b // 16]), g4[t][:, a:b], ALU.mult)
+            if not last:
+                chances(t + 1)
+            for a, b in parts:
+                nc.scalar.activation(u[:, a:b], u[:, a:b], ACT.Copy, bias=1.0)
+            if not last:
+                inner(t + 1)
+            for a, b in parts:
+                nc.vector.tensor_tensor(y_t[:, a:b], r[t][:].indirect(first[:, a // 16 : b // 16]), u[:, a:b], ALU.mult)
                 nc.sync.dma_start(out=out_rows[:, t, a:b], in_=y_t[:, a:b])
-                if t == 1:
-                    nc.scalar.copy(y_b[:, :, 0:2], y01[:].rearrange("p t j -> p j t"))
-                if t == 3:
-                    if a == 0:
-                        nc.scalar.copy(y_b[:, a:b, 2:4], y23[:, :, a:b].rearrange("p t j -> p j t"))
-                    else:
-                        nc.vector.tensor_copy(y_b[:, a:b, 2:4], y23[:, :, a:b].rearrange("p t j -> p j t"))
-                    nc.vector.quantize_mx(
-                        out=y_c[:, a:b].bitcast(FP8X4), scales=y_s[:, a:b], in_=y_b[:, a:b, :].rearrange("p j t -> p (j t)")
-                    )
-                    nc.scalar.dma_start(out=out_words[:, a:b], in_=y_c[:, a:b].bitcast(I32))
+            if t == 2:
+                nc.scalar.copy(y_b[:, :, 0:2], pairs[0][:].rearrange("p t j -> p j t"))
+        for a, b in parts:
+            if a == 0:
+                nc.scalar.copy(y_b[:, a:b, 2:4], pairs[1][:, :, a:b].rearrange("p t j -> p j t"))
+            else:
+                nc.vector.tensor_copy(y_b[:, a:b, 2:4], pairs[1][:, :, a:b].rearrange("p t j -> p j t"))
+        for a, b in parts:
+            nc.vector.quantize_mx(
+                out=y_c[:, a:b].bitcast(FP8X4), scales=y_s[:, a:b], in_=y_b[:, a:b, :].rearrange("p j t -> p (j t)")
+            )
+            nc.scalar.dma_start(out=out_words[:, a:b], in_=y_c[:, a:b].bitcast(I32))
         for quad in range(4):
             queue = nc.sync if quad % 2 == 0 else nc.scalar
             queue.dma_start(

from contextlib import ExitStack

import concourse.mybir as mybir

D, K, T, I, J, Q = 512, 512, 2048, 1024, 512, 512
FLOPS = 2 * Q * I * (D + K)

F32 = mybir.dt.float32
BF16 = mybir.dt.bfloat16
I32 = mybir.dt.int32
U32 = mybir.dt.uint32
U16 = mybir.dt.uint16
U8 = mybir.dt.uint8
FP8X4 = mybir.dt.float8_e4m3fn_x4
ALU = mybir.AluOpType
ACT = mybir.ActivationFunctionType

P = 128
PACK = 4
BANK = 512
HALF = J // 2
WHOLE_BANKS = ((0, BANK), (BANK, I))
FINE = ((0, BANK), (BANK, BANK + BANK // 2), (BANK + BANK // 2, I))


def load_scale_rows(queue, window, scales):
    for quad in range(4):
        queue.dma_start(
            out=window[32 * quad : 32 * quad + 4, :].bitcast(I32),
            in_=scales[0, 4 * quad : 4 * quad + 4, :].bitcast(I32),
        )


def tile_attend_acceptedlength_pl_kernel(
    tc, ht, hd, et_words, et_scales, ed_words, ed_scales, l1, l2, offs, offs2, offs3, offs4, out_0, out_1, out_2
):
    nc = tc.nc
    with ExitStack() as ctx:
        lists = ctx.enter_context(tc.tile_pool(name="lists", bufs=1))
        keep = ctx.enter_context(tc.tile_pool(name="keep", bufs=1))
        psum = ctx.enter_context(tc.psum_pool(name="psum", bufs=1))

        nodes = lists.tile([P, I // 16], U16, name="nodes")
        first = lists.tile([P, J // 16], U16, name="first")
        second = lists.tile([P, J // 16], U16, name="second")
        third = lists.tile([P, J // 16], U16, name="third")

        et_w = keep.tile([P, T], I32, name="et_w", align_bytes=64)
        ed_w = keep.tile([P, T], I32, name="ed_w", tag="ed_w_then_late_codes", align_bytes=64)
        et_s = keep.tile([P, T], U8, name="et_s", align_bytes=64)
        ed_s = keep.tile([P, T], U8, name="ed_s", tag="ed_s_then_early_s", align_bytes=64)
        ht_raw = keep.tile([P, PACK, Q], F32, name="ht_raw", align_bytes=64)
        hd_raw = keep.tile([P, PACK, Q], F32, name="hd_raw", align_bytes=64)
        l1_sb = keep.tile([P, PACK], F32, name="l1_sb")
        l2_sb = keep.tile([P, PACK], F32, name="l2_sb")

        nc.vector.memset(et_s[:].bitcast(I32), 0)
        nc.gpsimd.memset(ed_s[:].bitcast(I32), 0)
        nc.sync.dma_start(nodes[:], offs)
        load_scale_rows(nc.scalar, et_s, et_scales)
        warm = keep.tile([P, 2], F32, name="warm")
        nc.vector.memset(warm[:, 0:1], 0.0)
        nc.scalar.activation(warm[:, 1:2], warm[:, 0:1], ACT.Exp)
        nc.sync.dma_start(out=et_w[:], in_=et_words[0].rearrange("p n r -> p (n r)").bitcast(I32))
        nc.sync.dma_start(out=ht_raw[:], in_=ht.rearrange("(p j) q -> p j q", j=PACK))
        load_scale_rows(nc.sync, ed_s, ed_scales)
        nc.sync.dma_start(out=hd_raw[:], in_=hd.rearrange("(p j) q -> p j q", j=PACK))
        nc.sync.dma_start(out=ed_w[:], in_=ed_words[0].rearrange("p n r -> p (n r)").bitcast(I32))
        nc.gpsimd.dma_start(out=l1_sb[:], in_=l1.rearrange("(p t) o -> p (t o)", t=PACK))
        nc.gpsimd.dma_start(out=l2_sb[:], in_=l2.rearrange("(p t) o -> p (t o)", t=PACK))
        nc.sync.dma_start(third[:], offs4)
        nc.sync.dma_start(first[:], offs2)
        nc.sync.dma_start(second[:], offs3)

        et_gw = keep.tile([P, I], U32, name="et_gw", align_bytes=64)
        et_gs = keep.tile([P, I], U8, name="et_gs", align_bytes=64)
        ed_gs = keep.tile([P, I], U8, name="ed_gs", align_bytes=64)
        nc.vector.tensor_copy(et_gs[:], et_s[:].indirect(nodes[:]))
        nc.vector.tensor_copy(et_gw[:], et_w[:].bitcast(U32).indirect(nodes[:]))
        nc.vector.tensor_copy(ed_gs[:], ed_s[:].indirect(nodes[:]))

        shift = keep.tile([P, PACK], F32, name="shift")
        for t in range(PACK):
            nc.scalar.activation(shift[:, t : t + 1], l2_sb[:, t : t + 1], ACT.Identity, bias=l1_sb[:, t : t + 1], scale=-1.0)

        ht_b = keep.tile([P, PACK, P, PACK], BF16, name="ht_b", align_bytes=64)
        hd_b = [keep.tile([P, 2, P, PACK], BF16, name=f"hd_b{i}", align_bytes=64) for i in range(2)]
        hd_dealt = hd_raw[:].rearrange("p j (m t) -> p m j t", t=PACK)
        nc.scalar.activation(
            ht_b[:].rearrange("p t m j -> p m j t"), ht_raw[:].rearrange("p j (m t) -> p m j t", t=PACK), ACT.Copy
        )
        for i in range(2):
            nc.scalar.activation(
                hd_b[i][:].rearrange("p t m j -> p m j t"), hd_dealt[:, :, :, 2 * i : 2 * i + 2], ACT.Copy, scale=-1.0
            )

        def quantise(codes, scales, pair):
            nc.vector.quantize_mx(out=codes.bitcast(FP8X4), scales=scales, in_=pair.rearrange("p t m j -> p (t m j)"))
            return codes, scales

        ht01_c = keep.tile([P, 2 * P], U32, name="ht01_c", align_bytes=64)
        ht01_s = keep.tile([P, 2 * P], U8, name="ht01_s", tag="ed_s_then_early_s", align_bytes=64)
        hd01_c = keep.tile([P, 2 * P], U32, name="hd01_c", align_bytes=64)
        hd01_s = keep.tile([P, 2 * P], U8, name="hd01_s", align_bytes=64)
        target = [quantise(ht01_c[:], ht01_s[:], ht_b[:, 0:2])]
        draft = [quantise(hd01_c[:], hd01_s[:], hd_b[0][:])]
        ed_gw = keep.tile([P, I], U32, name="ed_gw", align_bytes=64)
        for a, b in FINE:
            nc.vector.tensor_copy(ed_gw[:, a:b], ed_w[:].bitcast(U32).indirect(nodes[:, a // 16 : b // 16]))

        r = [keep.tile([P, 2 * I], F32, name=f"r{t}", align_bytes=64) for t in range(PACK)]
        nc.vector.memset(r[0][:, I + BANK :], 0.0)

        def chances(t):
            pieces = FINE if t == 0 else WHOLE_BANKS
            if t == 0:
                banks = [psum.tile([P, b - a], F32, name=f"fine{a}") for a, b in pieces]
            else:
                banks = [psum.tile([P, b - a], F32, name=f"bank{a}", bufs=2) for a, b in pieces]
            for side, gw, gs in ((target, et_gw, et_gs), (draft, ed_gw, ed_gs)):
                codes, scales = side[t // 2]
                rows = slice(P * (t % 2), P * (t % 2 + 1))
                for bank, (a, b) in zip(banks, pieces):
                    nc.tensor.matmul_mx(
                        out=bank[:], lhsT=codes[:, rows].bitcast(FP8X4), lhsT_scale=scales[:, rows],
                        rhs=gw[:, a:b].bitcast(FP8X4), rhs_scale=gs[:, a:b],
                        start=side is target, stop=side is draft,
                    )
            for bank, (a, b) in zip(banks, pieces):
                if t == 0 and a > 0:
                    capped = r[1][:, BANK + a : BANK + b]
                    nc.vector.tensor_scalar(capped, bank[:], shift[:, t : t + 1], 0.0, ALU.subtract, ALU.min)
                    nc.scalar.activation(r[t][:, a:b], capped, ACT.Exp)
                else:
                    excess = r[t][:, I + a : I + b]
                    nc.scalar.activation(excess, bank[:], ACT.Relu, bias=shift[:, t : t + 1], scale=-1.0)
                    nc.scalar.activation(r[t][:, a:b], excess, ACT.Exp, scale=-1.0)

        y_b = keep.tile([P, J, PACK], BF16, name="y_b", align_bytes=64)
        y_c = keep.tile([P, J], U32, name="y_c", align_bytes=64)
        y_s = keep.tile([P, J], U8, name="y_s", align_bytes=64)
        out_rows = out_0.rearrange("(p t) j -> p t j", t=PACK)
        out_words = out_1[0].rearrange("p n r -> p (n r)").bitcast(I32)
        pairs = [keep.tile([P, 2, J], F32, name=f"y_pair{i}", align_bytes=64) for i in range(2)]
        g4 = [keep.tile([P, J], F32, name=f"g4{t}", align_bytes=64) for t in range(PACK)]

        def inner(t):
            nc.vector.tensor_scalar(g4[t][:], r[t][:].indirect(third[:]), 1.0, 1.0, ALU.mult, ALU.add)

        chances(0)
        late_c = keep.tile([P, 4 * P], U32, name="late_c", tag="ed_w_then_late_codes", align_bytes=64)
        late_s = keep.tile([P, 4 * P], U8, name="late_s", align_bytes=64)
        target.append(quantise(late_c[:, : 2 * P], late_s[:, : 2 * P], ht_b[:, 2:4]))
        draft.append(quantise(late_c[:, 2 * P :], late_s[:, 2 * P :], hd_b[1][:]))
        inner(0)
        for t in range(PACK):
            last = t == PACK - 1
            parts = ((0, HALF), (HALF, J)) if last else ((0, J),)
            u = keep.tile([P, J], F32, name="u", align_bytes=64)
            y_t = pairs[t // 2][:, t % 2, :]
            for a, b in parts:
                nc.vector.tensor_tensor(u[:, a:b], r[t][:].indirect(second[:, a // 16 : b // 16]), g4[t][:, a:b], ALU.mult)
            if not last:
                chances(t + 1)
            for a, b in parts:
                nc.scalar.activation(u[:, a:b], u[:, a:b], ACT.Copy, bias=1.0)
            if not last:
                inner(t + 1)
            for a, b in parts:
                nc.vector.tensor_tensor(y_t[:, a:b], r[t][:].indirect(first[:, a // 16 : b // 16]), u[:, a:b], ALU.mult)
                nc.sync.dma_start(out=out_rows[:, t, a:b], in_=y_t[:, a:b])
            if t == 2:
                nc.scalar.copy(y_b[:, :, 0:2], pairs[0][:].rearrange("p t j -> p j t"))
        for a, b in parts:
            if a == 0:
                nc.scalar.copy(y_b[:, a:b, 2:4], pairs[1][:, :, a:b].rearrange("p t j -> p j t"))
            else:
                nc.vector.tensor_copy(y_b[:, a:b, 2:4], pairs[1][:, :, a:b].rearrange("p t j -> p j t"))
        for a, b in parts:
            nc.vector.quantize_mx(
                out=y_c[:, a:b].bitcast(FP8X4), scales=y_s[:, a:b], in_=y_b[:, a:b, :].rearrange("p j t -> p (j t)")
            )
            nc.scalar.dma_start(out=out_words[:, a:b], in_=y_c[:, a:b].bitcast(I32))
        for quad in range(4):
            queue = nc.sync if quad % 2 == 0 else nc.scalar
            queue.dma_start(
                out=out_2[0, 4 * quad : 4 * quad + 4, :].bitcast(I32), in_=y_s[32 * quad : 32 * quad + 4, :].bitcast(I32)
            )
